import numpy as np
import ml_dtypes


def mxq(x, axis, fmt="e4m3"):
    dtype, down = {"e4m3": (ml_dtypes.float8_e4m3fn, 7), "e5m2": (ml_dtypes.float8_e5m2, 14)}[fmt]
    v = np.moveaxis(np.asarray(x, np.float32).astype(ml_dtypes.bfloat16).astype(np.float64), axis, -1)
    blocks = v.reshape(v.shape[:-1] + (-1, 32))
    amax = np.abs(blocks).max(-1, keepdims=True)
    byte = np.maximum(np.where(amax > 0, np.frexp(amax)[1] - 1 + 127, 0) - down, 1)
    scale = np.exp2(byte - 127.0)
    codes = (blocks / scale).astype(np.float32).astype(dtype).astype(np.float64)
    return np.moveaxis((codes * scale).reshape(v.shape), -1, axis)


WIDE = False


def mx_kscale(k):
    if not WIDE:
        return np.ones(k)
    levels = np.array([10, -10, 5, -5, 0])
    if k % 512:
        return np.exp2(np.random.permutation(np.resize(levels, k // 32))).repeat(32)
    a = np.empty((k // 512, 16))
    for p in range(k // 512):
        a[p, :8] = np.random.permutation(np.resize(levels, 8))
        for g in range(8):
            far = levels[np.abs(levels - a[p, g]) >= 10]
            a[p, g + 8] = far[np.random.randint(len(far))]
    return np.exp2(a.ravel()).repeat(32)


def f64(x):
    return np.asarray(x).astype(np.float64)


def striped(idx):
    return np.tile(np.asarray(idx).reshape(-1, 16).T, (8, 1)).astype(np.uint16)


def unstriped(offs):
    return offs[:16].T.reshape(-1).astype(np.int64)


E2M1 = np.array([0.0, 0.5, 1.0, 1.5, 2.0, 3.0, 4.0, 6.0, -0.0, -0.5, -1.0, -1.5, -2.0, -3.0, -4.0, -6.0])


def pack_weight(w, fmt):
    k, n = w.shape
    w = f64(np.asarray(w, np.float32).astype(ml_dtypes.bfloat16)).reshape(k // 32, 32, n)
    amax = np.abs(w).max(1)
    if fmt == "e4m3":
        byte = np.frexp(amax)[1] - 1 + 127 - 7
    else:
        mant, ex = np.frexp(amax / 6.0)
        byte = np.where(mant > 0.5, ex, ex - 1) + 127
    byte = np.clip(np.where(amax > 0, byte, 1), 1, 254)
    scaled = (w * np.exp2(127.0 - byte)[:, None, :]).reshape(k, n).astype(np.float32)
    by_word = np.ascontiguousarray(scaled.reshape(k // 512, 128, 4, n).transpose(0, 1, 3, 2))
    if fmt == "e4m3":
        words = by_word.astype(ml_dtypes.float8_e4m3fn).view(np.uint8)
    else:
        c = by_word.astype(ml_dtypes.float4_e2m1fn).view(np.uint8) & 0xF
        words = (c[..., 0::2] | (c[..., 1::2] << 4)).reshape(k // 512, 128, 2 * n)
    return np.ascontiguousarray(words), np.ascontiguousarray(byte.astype(np.uint8).reshape(k // 512, 16, n))


def unpack_weight(words, scales, fmt):
    g, _, n = scales.shape
    words = np.ascontiguousarray(words).reshape(g, 128, n, -1)
    if fmt == "e4m3":
        vals = words.view(ml_dtypes.float8_e4m3fn).astype(np.float64)
    else:
        nib = np.empty((g, 128, n, 4), np.uint8)
        nib[..., 0::2] = words & 0xF
        nib[..., 1::2] = words >> 4
        vals = E2M1[nib]
    vals = vals * np.repeat(np.exp2(scales.astype(np.float64) - 127.0), 8, axis=1)[..., None]
    return vals.transpose(0, 1, 3, 2).reshape(g * 512, n)


def softplus(v):
    return np.log(1.0 + np.exp(v))


K, L, T, J, N = 1024, 512, 1024, 512, 512


def setup_inputs():
    n = np.random.standard_normal
    idx = np.random.permutation(T)[:J]
    fk = mx_kscale(K)
    fl = mx_kscale(L)
    xtp = pack_weight(n((K, T)) / fk[:, None], "e4m3")
    wsp = pack_weight(n((K, N)) * 1 / np.sqrt(K) * fk[:, None], "e2m1")
    xep = pack_weight(n((L, J)) / fl[:, None], "e4m3")
    return {
        "xt_words": xtp[0],
        "xt_scales": xtp[1],
        "ws_words": wsp[0],
        "ws_scales": wsp[1],
        "xe_words": xep[0],
        "xe_scales": xep[1],
        "we": (n((L, N)) * 1 / np.sqrt(L) * fl[:, None]).astype(np.float32),
        "b": (np.random.uniform(-0.5, 0.5, (N, 1))).astype(np.float32),
        "offs": striped(idx),
    }


def reference(xt_words, xt_scales, ws_words, ws_scales, xe_words, xe_scales, we, b, offs):
    idx = unstriped(offs)
    xtu = unpack_weight(xt_words, xt_scales, "e4m3")
    wsu = unpack_weight(ws_words, ws_scales, "e2m1")
    xeu = unpack_weight(xe_words, xe_scales, "e4m3")
    u = wsu.T @ xtu
    weq = mxq(f64(we), 0, "e4m3")
    p = weq.T @ xeu
    d = softplus(p - u[:, idx])
    dp = np.zeros((N, T))
    dp[:, idx] = d
    y = u + dp + f64(b)
    return y

@@ -1,0 +1,221 @@
+from contextlib import ExitStack
+
+import concourse.mybir as mybir
+
+K, L, T, J, N = 1024, 512, 1024, 512, 512
+FLOPS = 2 * K * T * N + 2 * L * J * N
+
+F32 = mybir.dt.float32
+BF16 = mybir.dt.bfloat16
+I32 = mybir.dt.int32
+U32 = mybir.dt.uint32
+U16 = mybir.dt.uint16
+U8 = mybir.dt.uint8
+FP8X4 = mybir.dt.float8_e4m3fn_x4
+FP4X4 = mybir.dt.float4_e2m1fn_x4
+ACT = mybir.ActivationFunctionType
+ALU = mybir.AluOpType
+
+P = 128
+PACK = 4
+PASSES = K // (P * PACK)
+BANK = 512
+BLOCKS = N // P
+HALVES = T // BANK
+PAIR = 2
+OVERLAP = 16
+
+
+def tile_moe_smooth_larger_of_expert_and_shared_kernel(
+    tc, xt_words, xt_scales, ws_words, ws_scales, xe_words, xe_scales, we, b, offs, out
+):
+    nc = tc.nc
+    with ExitStack() as ctx:
+        keep = ctx.enter_context(tc.tile_pool(name="keep", bufs=1))
+        psum = ctx.enter_context(tc.psum_pool(name="psum", bufs=1))
+
+        xt_plane = keep.tile([P, PASSES, T], U8, align_bytes=64)
+        ws_plane = keep.tile([P, PASSES, N], U8, align_bytes=64)
+        xe_plane = keep.tile([P, 1, J], U8, align_bytes=64)
+        nc.gpsimd.memset(xt_plane[:].bitcast(I32), 0)
+        nc.vector.memset(ws_plane[:].bitcast(I32), 0)
+        nc.gpsimd.memset(xe_plane[:].bitcast(I32), 0)
+
+        we_view = we.rearrange("(p j) c -> p j c", j=PACK)
+        pair_cols = PAIR * P
+        xe_codes = keep.tile([P, J], U32, align_bytes=64)
+        ws_codes = keep.tile([P, PASSES, 2 * N], U8, align_bytes=64)
+        xt_codes = [keep.tile([P, PASSES, BANK], U32, name=f"xt_codes{h}", align_bytes=64) for h in range(HALVES)]
+        xt_view = xt_words.rearrange("z p t r -> p z (t r)")
+        offsets = keep.tile([P, J // 16], U16)
+
+        def load_scales(queue, plane, scales):
+            rows = scales.rearrange("z (q r) n -> r q z n", r=4)
+            for r in range(4):
+                queue.dma_start(plane[r:P:32].bitcast(I32), rows[r].bitcast(I32))
+
+        def load_we(g):
+            raw = keep.tile([P, PACK, pair_cols], F32, name=f"we_raw{g}", tag="we_raw")
+            nc.sync.dma_start(raw[:], we_view[:, :, g * pair_cols : (g + 1) * pair_cols])
+            return raw
+
+        def load_xt(h):
+            nc.sync.dma_start(
+                xt_codes[h][:].bitcast(I32), xt_view[:, :, h * BANK * PACK : (h + 1) * BANK * PACK].bitcast(I32)
+            )
+
+        nc.sync.dma_start(ws_codes[:].bitcast(I32), ws_words.rearrange("z p c -> p z c").bitcast(I32))
+        load_scales(nc.sync, xt_plane, xt_scales)
+        raw0 = load_we(0)
+        load_xt(0)
+        nc.sync.dma_start(xe_codes[:].bitcast(I32), xe_words[0].rearrange("p t r -> p (t r)").bitcast(I32))
+        load_scales(nc.sync, ws_plane, ws_scales)
+        load_xt(1)
+        load_scales(nc.sync, xe_plane, xe_scales)
+        nc.sync.dma_start(offsets[:], offs)
+
+        dp = [keep.tile([P, T], F32, name=f"dp{i}") for i in range(PAIR)]
+        for i in range(PAIR):
+            nc.vector.memset(dp[i][:], 0.0)
+
+        we_codes = keep.tile([P, N], U32, align_bytes=64)
+        we_plane = keep.tile([P, N], U8, align_bytes=64)
+
+        def quantize_we(g, raw, tag):
+            cols = slice(g * pair_cols, (g + 1) * pair_cols)
+            grouped = keep.tile([P, pair_cols, PACK], BF16, name=f"grouped{g}", tag=tag, align_bytes=64)
+            nc.vector.tensor_copy(
+                grouped[:].rearrange("p (c i) t -> p c t i", i=4),
+                raw[:].rearrange("p t (c i) -> p c t i", i=4),
+            )
+            nc.vector.quantize_mx(
+                out=we_codes[:, cols].bitcast(FP8X4),
+                scales=we_plane[:, cols],
+                in_=grouped[:].rearrange("p c t -> p (c t)"),
+            )
+
+        u, p_sb, lin, ex = {}, {}, {}, {}
+
+        def new(store, key, cols, tag):
+            store[key] = keep.tile([P, cols], F32, name=f"{tag}_{key}", tag=tag, align_bytes=64)
+
+        y = [keep.tile([P, J], F32, name=f"y{i}") for i in range(BLOCKS)]
+        mag = [keep.tile([P, J], F32, name=f"mag{i}") for i in range(BLOCKS)]
+        lg = [keep.tile([P, PAIR * J], F32, name=f"lg{g}") for g in range(BLOCKS // PAIR)]
+        res = [keep.tile([P, T], F32, name=f"res{i}") for i in range(BLOCKS)]
+
+        def copy_out(engine, dst, src):
+            if engine == "scalar":
+                nc.scalar.activation(dst, src, ACT.Copy)
+            else:
+                nc.vector.tensor_copy(dst, src)
+
+        def shared_half(i, h, engine, bank):
+            acc = psum.tile([P, BANK], F32, name="acc", tag=f"bank{bank}")
+            for z in range(PASSES):
+                nc.tensor.matmul_mx(
+                    out=acc[:],
+                    lhsT=ws_codes[:, z, i * 2 * P : (i + 1) * 2 * P].bitcast(FP4X4),
+                    lhsT_scale=ws_plane[:, z, i * P : (i + 1) * P],
+                    rhs=xt_codes[h][:, z, :].bitcast(FP8X4),
+                    rhs_scale=xt_plane[:, z, h * BANK : (h + 1) * BANK],
+                    start=(z == 0),
+                    stop=(z == PASSES - 1),
+                )
+            copy_out(engine, u[i][:, h * BANK : (h + 1) * BANK], acc[:])
+
+        def expert(i, engine, bank):
+            acc = psum.tile([P, BANK], F32, name="acc", tag=f"bank{bank}")
+            nc.tensor.matmul_mx(
+                out=acc[:],
+                lhsT=we_codes[:, i * P : (i + 1) * P].bitcast(FP8X4),
+                lhsT_scale=we_plane[:, i * P : (i + 1) * P],
+                rhs=xe_codes[:].bitcast(FP8X4),
+                rhs_scale=xe_plane[:, 0, :],
+                start=True,
+                stop=True,
+            )
+            copy_out(engine, p_sb[i][:], acc[:])
+
+        def gather(i):
+            nc.vector.tensor_tensor(y[i][:], u[i][:].indirect(offsets[:]), p_sb[i][:], ALU.subtract)
+
+        def exp_part(i):
+            g, s = divmod(i, PAIR)
+            nc.scalar.activation(mag[i][:], y[i][:], ACT.Abs)
+            nc.scalar.activation(ex[g][:, s * J : (s + 1) * J], mag[i][:], ACT.Exp, scale=-1.0)
+
+        def log_part(g):
+            for cols in (slice(0, J + OVERLAP), slice(J + OVERLAP, PAIR * J)):
+                nc.scalar.activation(lg[g][:, cols], ex[g][:, cols], ACT.Ln, bias=1.0)
+
+        def linear_part(i, engine):
+            if engine == "scalar":
+                nc.scalar.activation(lin[i][:], y[i][:], ACT.Relu, scale=-1.0)
+            else:
+                nc.vector.tensor_scalar(lin[i][:], y[i][:], -1.0, 0.0, ALU.mult, ALU.max)
+
+        def scatter(i):
+            g, s = divmod(i, PAIR)
+            nc.vector.tensor_tensor(dp[s][:].indirect(offsets[:]), lg[g][:, s * J : (s + 1) * J], lin[i][:], ALU.add)
+
+        def finish(i, pieces):
+            width = T // pieces
+            for c in range(pieces):
+                cols = slice(c * width, (c + 1) * width)
+                nc.vector.scalar_tensor_tensor(
+                    res[i][:, cols], u[i][:, cols], bias[:, i : i + 1], dp[i % PAIR][:, cols], ALU.add, ALU.add
+                )
+                nc.sync.dma_start(out[i * P : (i + 1) * P, cols], res[i][:, cols])
+
+        for i in range(3):
+            new(u, i, T, f"u{i}")
+            new(p_sb, i, J, f"p{i}")
+        for g in range(2):
+            new(ex, g, PAIR * J, f"ex{g}")
+        for i in (0, 2, 3):
+            new(lin, i, J, f"lin{i}")
+
+        quantize_we(0, raw0, "grouped")
+        raw1 = load_we(1)
+        bias = keep.tile([P, BLOCKS], F32, tag="grouped", align_bytes=64)
+        with nc.allow_non_contiguous_dma(reason="one bias value a partition"):
+            nc.sync.dma_start(bias[:], b.rearrange("(c p) o -> p (c o)", p=P))
+        shared_half(0, 0, "scalar", 1)
+        shared_half(1, 0, "vector", 3)
+        shared_half(0, 1, "vector", 4)
+        expert(0, "scalar", 0)
+        expert(1, "scalar", 2)
+        shared_half(1, 1, "scalar", 5)
+        gather(0)
+        shared_half(2, 0, "scalar", 6)
+        gather(1)
+        exp_part(0)
+        exp_part(1)
+        quantize_we(1, raw1, "p1")
+        shared_half(2, 1, "vector", 7)
+        linear_part(0, "vector")
+        expert(2, "vector", 0)
+        log_part(0)
+        gather(2)
+        new(u, 3, T, "ex0")
+        new(p_sb, 3, J, "p3")
+        shared_half(3, 0, "scalar", 1)
+        shared_half(3, 1, "scalar", 2)
+        expert(3, "scalar", 1)
+        scatter(0)
+        gather(3)
+        new(lin, 1, J, "p3")
+        linear_part(1, "vector")
+        linear_part(2, "scalar")
+        exp_part(2)
+        exp_part(3)
+        finish(0, 1)
+        scatter(1)
+        log_part(1)
+        linear_part(3, "scalar")
+        finish(1, 1)
+        scatter(2)
+        finish(2, 1)
+        scatter(3)
+        finish(3, 2)

@@ -37,9 +37,9 @@ def tile_moe_smooth_larger_of_expert_and_shared_kernel(
         xt_plane = keep.tile([P, PASSES, T], U8, align_bytes=64)
         ws_plane = keep.tile([P, PASSES, N], U8, align_bytes=64)
         xe_plane = keep.tile([P, 1, J], U8, align_bytes=64)
-        nc.gpsimd.memset(xt_plane[:].bitcast(I32), 0)
-        nc.vector.memset(ws_plane[:].bitcast(I32), 0)
         nc.gpsimd.memset(xe_plane[:].bitcast(I32), 0)
+        nc.vector.memset(ws_plane[:].bitcast(I32), 0)
+        nc.vector.memset(xt_plane[:].bitcast(I32), 0)
 
         we_view = we.rearrange("(p j) c -> p j c", j=PACK)
         pair_cols = PAIR * P
@@ -49,9 +49,9 @@ def tile_moe_smooth_larger_of_expert_and_shared_kernel(
         xt_view = xt_words.rearrange("z p t r -> p z (t r)")
         offsets = keep.tile([P, J // 16], U16)
 
-        def load_scales(queue, plane, scales):
+        def load_scales(queue, plane, scales, which):
             rows = scales.rearrange("z (q r) n -> r q z n", r=4)
-            for r in range(4):
+            for r in which:
                 queue.dma_start(plane[r:P:32].bitcast(I32), rows[r].bitcast(I32))
 
         def load_we(g):
@@ -64,19 +64,23 @@ def tile_moe_smooth_larger_of_expert_and_shared_kernel(
                 xt_codes[h][:].bitcast(I32), xt_view[:, :, h * BANK * PACK : (h + 1) * BANK * PACK].bitcast(I32)
             )
 
-        nc.sync.dma_start(ws_codes[:].bitcast(I32), ws_words.rearrange("z p c -> p z c").bitcast(I32))
-        load_scales(nc.sync, xt_plane, xt_scales)
+        bias = keep.tile([P, BLOCKS], F32)
+        warm = keep.tile([P, 16], F32)
+        nc.vector.memset(warm[:, 0:1], 0.0)
+        nc.scalar.activation(warm[:, 8:9], warm[:, 0:1], ACT.Exp)
+        with nc.allow_non_contiguous_dma(reason="one bias value a partition"):
+            nc.sync.dma_start(bias[:], b.rearrange("(c p) o -> p (c o)", p=P))
         raw0 = load_we(0)
-        load_xt(0)
+        load_scales(nc.sync, xe_plane, xe_scales, (0, 1))
+        load_scales(nc.gpsimd, xe_plane, xe_scales, (2, 3))
         nc.sync.dma_start(xe_codes[:].bitcast(I32), xe_words[0].rearrange("p t r -> p (t r)").bitcast(I32))
-        load_scales(nc.sync, ws_plane, ws_scales)
+        nc.sync.dma_start(ws_codes[:].bitcast(I32), ws_words.rearrange("z p c -> p z c").bitcast(I32))
+        load_scales(nc.sync, ws_plane, ws_scales, (0, 1))
+        load_xt(0)
+        load_scales(nc.sync, ws_plane, ws_scales, (2, 3))
+        load_scales(nc.sync, xt_plane, xt_scales, (0, 1, 2, 3))
         load_xt(1)
-        load_scales(nc.sync, xe_plane, xe_scales)
         nc.sync.dma_start(offsets[:], offs)
-
-        dp = [keep.tile([P, T], F32, name=f"dp{i}") for i in range(PAIR)]
-        for i in range(PAIR):
-            nc.vector.memset(dp[i][:], 0.0)
 
         we_codes = keep.tile([P, N], U32, align_bytes=64)
         we_plane = keep.tile([P, N], U8, align_bytes=64)
@@ -94,21 +98,19 @@ def tile_moe_smooth_larger_of_expert_and_shared_kernel(
                 in_=grouped[:].rearrange("p c t -> p (c t)"),
             )
 
-        u, p_sb, lin, ex = {}, {}, {}, {}
+        u, p_sb, y, neg_d, ex, dp, res = {}, {}, {}, {}, {}, {}, {}
 
         def new(store, key, cols, tag):
             store[key] = keep.tile([P, cols], F32, name=f"{tag}_{key}", tag=tag, align_bytes=64)
 
-        y = [keep.tile([P, J], F32, name=f"y{i}") for i in range(BLOCKS)]
         mag = [keep.tile([P, J], F32, name=f"mag{i}") for i in range(BLOCKS)]
         lg = [keep.tile([P, PAIR * J], F32, name=f"lg{g}") for g in range(BLOCKS // PAIR)]
-        res = [keep.tile([P, T], F32, name=f"res{i}") for i in range(BLOCKS)]
 
-        def copy_out(engine, dst, src):
+        def copy_out(engine, dst, src, i):
             if engine == "scalar":
-                nc.scalar.activation(dst, src, ACT.Copy)
+                nc.scalar.activation(dst, src, ACT.Identity, bias=bias[:, i : i + 1])
             else:
-                nc.vector.tensor_copy(dst, src)
+                nc.vector.tensor_scalar(dst, src, bias[:, i : i + 1], None, ALU.add)
 
         def shared_half(i, h, engine, bank):
             acc = psum.tile([P, BANK], F32, name="acc", tag=f"bank{bank}")
@@ -122,7 +124,7 @@ def tile_moe_smooth_larger_of_expert_and_shared_kernel(
                     start=(z == 0),
                     stop=(z == PASSES - 1),
                 )
-            copy_out(engine, u[i][:, h * BANK : (h + 1) * BANK], acc[:])
+            copy_out(engine, u[i][:, h * BANK : (h + 1) * BANK], acc[:], i)
 
         def expert(i, engine, bank):
             acc = psum.tile([P, BANK], F32, name="acc", tag=f"bank{bank}")
@@ -135,7 +137,7 @@ def tile_moe_smooth_larger_of_expert_and_shared_kernel(
                 start=True,
                 stop=True,
             )
-            copy_out(engine, p_sb[i][:], acc[:])
+            copy_out(engine, p_sb[i][:], acc[:], i)
 
         def gather(i):
             nc.vector.tensor_tensor(y[i][:], u[i][:].indirect(offsets[:]), p_sb[i][:], ALU.subtract)
@@ -149,73 +151,70 @@ def tile_moe_smooth_larger_of_expert_and_shared_kernel(
             for cols in (slice(0, J + OVERLAP), slice(J + OVERLAP, PAIR * J)):
                 nc.scalar.activation(lg[g][:, cols], ex[g][:, cols], ACT.Ln, bias=1.0)
 
-        def linear_part(i, engine):
-            if engine == "scalar":
-                nc.scalar.activation(lin[i][:], y[i][:], ACT.Relu, scale=-1.0)
-            else:
-                nc.vector.tensor_scalar(lin[i][:], y[i][:], -1.0, 0.0, ALU.mult, ALU.max)
-
         def scatter(i):
             g, s = divmod(i, PAIR)
-            nc.vector.tensor_tensor(dp[s][:].indirect(offsets[:]), lg[g][:, s * J : (s + 1) * J], lin[i][:], ALU.add)
+            nc.vector.scalar_tensor_tensor(
+                neg_d[i][:], y[i][:], 0.0, lg[g][:, s * J : (s + 1) * J], ALU.min, ALU.subtract
+            )
+            nc.vector.tensor_copy(dp[s][:].indirect(offsets[:]), neg_d[i][:])
 
-        def finish(i, pieces):
-            width = T // pieces
-            for c in range(pieces):
-                cols = slice(c * width, (c + 1) * width)
-                nc.vector.scalar_tensor_tensor(
-                    res[i][:, cols], u[i][:, cols], bias[:, i : i + 1], dp[i % PAIR][:, cols], ALU.add, ALU.add
-                )
-                nc.sync.dma_start(out[i * P : (i + 1) * P, cols], res[i][:, cols])
+        def finish(engine, i, cols):
+            engine.tensor_tensor(res[i][:, cols], u[i][:, cols], dp[i % PAIR][:, cols], ALU.subtract)
+            nc.sync.dma_start(out[i * P : (i + 1) * P, cols], res[i][:, cols])
 
         for i in range(3):
             new(u, i, T, f"u{i}")
             new(p_sb, i, J, f"p{i}")
+        for i in range(BLOCKS):
+            new(y, i, J, f"y{i}")
         for g in range(2):
             new(ex, g, PAIR * J, f"ex{g}")
         for i in (0, 2, 3):
-            new(lin, i, J, f"lin{i}")
+            new(neg_d, i, J, f"neg_d{i}")
+        whole = slice(0, T)
 
         quantize_we(0, raw0, "grouped")
         raw1 = load_we(1)
-        bias = keep.tile([P, BLOCKS], F32, tag="grouped", align_bytes=64)
-        with nc.allow_non_contiguous_dma(reason="one bias value a partition"):
-            nc.sync.dma_start(bias[:], b.rearrange("(c p) o -> p (c o)", p=P))
-        shared_half(0, 0, "scalar", 1)
-        shared_half(1, 0, "vector", 3)
-        shared_half(0, 1, "vector", 4)
+        new(dp, 0, T, "grouped")
+        nc.vector.memset(dp[0][:], 0.0)
         expert(0, "scalar", 0)
-        expert(1, "scalar", 2)
-        shared_half(1, 1, "scalar", 5)
+        expert(1, "scalar", 1)
+        shared_half(0, 0, "scalar", 2)
+        shared_half(0, 1, "vector", 3)
+        shared_half(1, 0, "scalar", 0)
+        shared_half(1, 1, "scalar", 4)
         gather(0)
-        shared_half(2, 0, "scalar", 6)
+        new(dp, 1, T, "p0")
+        nc.gpsimd.memset(dp[1][:], 0.0)
         gather(1)
         exp_part(0)
         exp_part(1)
         quantize_we(1, raw1, "p1")
-        shared_half(2, 1, "vector", 7)
-        linear_part(0, "vector")
-        expert(2, "vector", 0)
+        shared_half(2, 0, "vector", 3)
+        shared_half(2, 1, "vector", 4)
+        expert(2, "vector", 5)
         log_part(0)
         gather(2)
         new(u, 3, T, "ex0")
         new(p_sb, 3, J, "p3")
-        shared_half(3, 0, "scalar", 1)
-        shared_half(3, 1, "scalar", 2)
-        expert(3, "scalar", 1)
+        shared_half(3, 0, "scalar", 6)
+        shared_half(3, 1, "scalar", 7)
         scatter(0)
+        expert(3, "vector", 6)
         gather(3)
-        new(lin, 1, J, "p3")
-        linear_part(1, "vector")
-        linear_part(2, "scalar")
+        new(neg_d, 1, J, "p3")
         exp_part(2)
         exp_part(3)
-        finish(0, 1)
         scatter(1)
         log_part(1)
-        linear_part(3, "scalar")
-        finish(1, 1)
+        new(res, 0, T, "y1")
+        finish(nc.gpsimd, 0, whole)
         scatter(2)
-        finish(2, 1)
+        new(res, 1, T, "y2")
+        finish(nc.gpsimd, 1, whole)
         scatter(3)
-        finish(3, 2)
+        new(res, 2, T, "y3")
+        finish(nc.gpsimd, 2, whole)
+        new(res, 3, T, "res3")
+        finish(nc.vector, 3, slice(0, BANK))
+        finish(nc.vector, 3, slice(BANK, T))

from contextlib import ExitStack

import concourse.mybir as mybir

K, L, T, J, N = 1024, 512, 1024, 512, 512
FLOPS = 2 * K * T * N + 2 * L * J * N

F32 = mybir.dt.float32
BF16 = mybir.dt.bfloat16
I32 = mybir.dt.int32
U32 = mybir.dt.uint32
U16 = mybir.dt.uint16
U8 = mybir.dt.uint8
FP8X4 = mybir.dt.float8_e4m3fn_x4
FP4X4 = mybir.dt.float4_e2m1fn_x4
ACT = mybir.ActivationFunctionType
ALU = mybir.AluOpType

P = 128
PACK = 4
PASSES = K // (P * PACK)
BANK = 512
BLOCKS = N // P
HALVES = T // BANK
PAIR = 2
OVERLAP = 16


def tile_moe_smooth_larger_of_expert_and_shared_kernel(
    tc, xt_words, xt_scales, ws_words, ws_scales, xe_words, xe_scales, we, b, offs, out
):
    nc = tc.nc
    with ExitStack() as ctx:
        keep = ctx.enter_context(tc.tile_pool(name="keep", bufs=1))
        psum = ctx.enter_context(tc.psum_pool(name="psum", bufs=1))

        xt_plane = keep.tile([P, PASSES, T], U8, align_bytes=64)
        ws_plane = keep.tile([P, PASSES, N], U8, align_bytes=64)
        xe_plane = keep.tile([P, 1, J], U8, align_bytes=64)
        nc.gpsimd.memset(xe_plane[:].bitcast(I32), 0)
        nc.vector.memset(ws_plane[:].bitcast(I32), 0)
        nc.vector.memset(xt_plane[:].bitcast(I32), 0)

        we_view = we.rearrange("(p j) c -> p j c", j=PACK)
        pair_cols = PAIR * P
        xe_codes = keep.tile([P, J], U32, align_bytes=64)
        ws_codes = keep.tile([P, PASSES, 2 * N], U8, align_bytes=64)
        xt_codes = [keep.tile([P, PASSES, BANK], U32, name=f"xt_codes{h}", align_bytes=64) for h in range(HALVES)]
        xt_view = xt_words.rearrange("z p t r -> p z (t r)")
        offsets = keep.tile([P, J // 16], U16)

        def load_scales(queue, plane, scales, which):
            rows = scales.rearrange("z (q r) n -> r q z n", r=4)
            for r in which:
                queue.dma_start(plane[r:P:32].bitcast(I32), rows[r].bitcast(I32))

        def load_we(g):
            raw = keep.tile([P, PACK, pair_cols], F32, name=f"we_raw{g}", tag="we_raw")
            nc.sync.dma_start(raw[:], we_view[:, :, g * pair_cols : (g + 1) * pair_cols])
            return raw

        def load_xt(h):
            nc.sync.dma_start(
                xt_codes[h][:].bitcast(I32), xt_view[:, :, h * BANK * PACK : (h + 1) * BANK * PACK].bitcast(I32)
            )

        bias = keep.tile([P, BLOCKS], F32)
        warm = keep.tile([P, 16], F32)
        nc.vector.memset(warm[:, 0:1], 0.0)
        nc.scalar.activation(warm[:, 8:9], warm[:, 0:1], ACT.Exp)
        with nc.allow_non_contiguous_dma(reason="one bias value a partition"):
            nc.sync.dma_start(bias[:], b.rearrange("(c p) o -> p (c o)", p=P))
        raw0 = load_we(0)
        load_scales(nc.sync, xe_plane, xe_scales, (0, 1))
        load_scales(nc.gpsimd, xe_plane, xe_scales, (2, 3))
        nc.sync.dma_start(xe_codes[:].bitcast(I32), xe_words[0].rearrange("p t r -> p (t r)").bitcast(I32))
        nc.sync.dma_start(ws_codes[:].bitcast(I32), ws_words.rearrange("z p c -> p z c").bitcast(I32))
        load_scales(nc.sync, ws_plane, ws_scales, (0, 1))
        load_xt(0)
        load_scales(nc.sync, ws_plane, ws_scales, (2, 3))
        load_scales(nc.sync, xt_plane, xt_scales, (0, 1, 2, 3))
        load_xt(1)
        nc.sync.dma_start(offsets[:], offs)

        we_codes = keep.tile([P, N], U32, align_bytes=64)
        we_plane = keep.tile([P, N], U8, align_bytes=64)

        def quantize_we(g, raw, tag):
            cols = slice(g * pair_cols, (g + 1) * pair_cols)
            grouped = keep.tile([P, pair_cols, PACK], BF16, name=f"grouped{g}", tag=tag, align_bytes=64)
            nc.vector.tensor_copy(
                grouped[:].rearrange("p (c i) t -> p c t i", i=4),
                raw[:].rearrange("p t (c i) -> p c t i", i=4),
            )
            nc.vector.quantize_mx(
                out=we_codes[:, cols].bitcast(FP8X4),
                scales=we_plane[:, cols],
                in_=grouped[:].rearrange("p c t -> p (c t)"),
            )

        u, p_sb, y, neg_d, ex, dp, res = {}, {}, {}, {}, {}, {}, {}

        def new(store, key, cols, tag):
            store[key] = keep.tile([P, cols], F32, name=f"{tag}_{key}", tag=tag, align_bytes=64)

        mag = [keep.tile([P, J], F32, name=f"mag{i}") for i in range(BLOCKS)]
        lg = [keep.tile([P, PAIR * J], F32, name=f"lg{g}") for g in range(BLOCKS // PAIR)]

        def copy_out(engine, dst, src, i):
            if engine == "scalar":
                nc.scalar.activation(dst, src, ACT.Identity, bias=bias[:, i : i + 1])
            else:
                nc.vector.tensor_scalar(dst, src, bias[:, i : i + 1], None, ALU.add)

        def shared_half(i, h, engine, bank):
            acc = psum.tile([P, BANK], F32, name="acc", tag=f"bank{bank}")
            for z in range(PASSES):
                nc.tensor.matmul_mx(
                    out=acc[:],
                    lhsT=ws_codes[:, z, i * 2 * P : (i + 1) * 2 * P].bitcast(FP4X4),
                    lhsT_scale=ws_plane[:, z, i * P : (i + 1) * P],
                    rhs=xt_codes[h][:, z, :].bitcast(FP8X4),
                    rhs_scale=xt_plane[:, z, h * BANK : (h + 1) * BANK],
                    start=(z == 0),
                    stop=(z == PASSES - 1),
                )
            copy_out(engine, u[i][:, h * BANK : (h + 1) * BANK], acc[:], i)

        def expert(i, engine, bank):
            acc = psum.tile([P, BANK], F32, name="acc", tag=f"bank{bank}")
            nc.tensor.matmul_mx(
                out=acc[:],
                lhsT=we_codes[:, i * P : (i + 1) * P].bitcast(FP8X4),
                lhsT_scale=we_plane[:, i * P : (i + 1) * P],
                rhs=xe_codes[:].bitcast(FP8X4),
                rhs_scale=xe_plane[:, 0, :],
                start=True,
                stop=True,
            )
            copy_out(engine, p_sb[i][:], acc[:], i)

        def gather(i):
            nc.vector.tensor_tensor(y[i][:], u[i][:].indirect(offsets[:]), p_sb[i][:], ALU.subtract)

        def exp_part(i):
            g, s = divmod(i, PAIR)
            nc.scalar.activation(mag[i][:], y[i][:], ACT.Abs)
            nc.scalar.activation(ex[g][:, s * J : (s + 1) * J], mag[i][:], ACT.Exp, scale=-1.0)

        def log_part(g):
            for cols in (slice(0, J + OVERLAP), slice(J + OVERLAP, PAIR * J)):
                nc.scalar.activation(lg[g][:, cols], ex[g][:, cols], ACT.Ln, bias=1.0)

        def scatter(i):
            g, s = divmod(i, PAIR)
            nc.vector.scalar_tensor_tensor(
                neg_d[i][:], y[i][:], 0.0, lg[g][:, s * J : (s + 1) * J], ALU.min, ALU.subtract
            )
            nc.vector.tensor_copy(dp[s][:].indirect(offsets[:]), neg_d[i][:])

        def finish(engine, i, cols):
            engine.tensor_tensor(res[i][:, cols], u[i][:, cols], dp[i % PAIR][:, cols], ALU.subtract)
            nc.sync.dma_start(out[i * P : (i + 1) * P, cols], res[i][:, cols])

        for i in range(3):
            new(u, i, T, f"u{i}")
            new(p_sb, i, J, f"p{i}")
        for i in range(BLOCKS):
            new(y, i, J, f"y{i}")
        for g in range(2):
            new(ex, g, PAIR * J, f"ex{g}")
        for i in (0, 2, 3):
            new(neg_d, i, J, f"neg_d{i}")
        whole = slice(0, T)

        quantize_we(0, raw0, "grouped")
        raw1 = load_we(1)
        new(dp, 0, T, "grouped")
        nc.vector.memset(dp[0][:], 0.0)
        expert(0, "scalar", 0)
        expert(1, "scalar", 1)
        shared_half(0, 0, "scalar", 2)
        shared_half(0, 1, "vector", 3)
        shared_half(1, 0, "scalar", 0)
        shared_half(1, 1, "scalar", 4)
        gather(0)
        new(dp, 1, T, "p0")
        nc.gpsimd.memset(dp[1][:], 0.0)
        gather(1)
        exp_part(0)
        exp_part(1)
        quantize_we(1, raw1, "p1")
        shared_half(2, 0, "vector", 3)
        shared_half(2, 1, "vector", 4)
        expert(2, "vector", 5)
        log_part(0)
        gather(2)
        new(u, 3, T, "ex0")
        new(p_sb, 3, J, "p3")
        shared_half(3, 0, "scalar", 6)
        shared_half(3, 1, "scalar", 7)
        scatter(0)
        expert(3, "vector", 6)
        gather(3)
        new(neg_d, 1, J, "p3")
        exp_part(2)
        exp_part(3)
        scatter(1)
        log_part(1)
        new(res, 0, T, "y1")
        finish(nc.gpsimd, 0, whole)
        scatter(2)
        new(res, 1, T, "y2")
        finish(nc.gpsimd, 1, whole)
        scatter(3)
        new(res, 2, T, "y3")
        finish(nc.gpsimd, 2, whole)
        new(res, 3, T, "res3")
        finish(nc.vector, 3, slice(0, BANK))
        finish(nc.vector, 3, slice(BANK, T))
